import numpy as np
import ml_dtypes


def mxq(x, axis, fmt="e4m3"):
    dtype, down = {"e4m3": (ml_dtypes.float8_e4m3fn, 7), "e5m2": (ml_dtypes.float8_e5m2, 14)}[fmt]
    v = np.moveaxis(np.asarray(x, np.float32).astype(ml_dtypes.bfloat16).astype(np.float64), axis, -1)
    blocks = v.reshape(v.shape[:-1] + (-1, 32))
    amax = np.abs(blocks).max(-1, keepdims=True)
    byte = np.maximum(np.where(amax > 0, np.frexp(amax)[1] - 1 + 127, 0) - down, 1)
    scale = np.exp2(byte - 127.0)
    codes = (blocks / scale).astype(np.float32).astype(dtype).astype(np.float64)
    return np.moveaxis((codes * scale).reshape(v.shape), -1, axis)


WIDE = False


def mx_kscale(k):
    if not WIDE:
        return np.ones(k)
    levels = np.array([30, -30])
    if k % 512:
        return np.exp2(np.random.permutation(np.resize(levels, k // 32))).repeat(32)
    a = np.empty((k // 512, 16))
    for p in range(k // 512):
        a[p, :8] = np.random.permutation(np.resize(levels, 8))
        for g in range(8):
            far = levels[np.abs(levels - a[p, g]) >= 10]
            a[p, g + 8] = far[np.random.randint(len(far))]
    return np.exp2(a.ravel()).repeat(32)


def f64(x):
    return np.asarray(x).astype(np.float64)


def striped(idx):
    return np.tile(np.asarray(idx).reshape(-1, 16).T, (8, 1)).astype(np.uint16)


def unstriped(offs):
    return offs[:16].T.reshape(-1).astype(np.int64)


E2M1 = np.array([0.0, 0.5, 1.0, 1.5, 2.0, 3.0, 4.0, 6.0, -0.0, -0.5, -1.0, -1.5, -2.0, -3.0, -4.0, -6.0])


def pack_weight(w, fmt):
    k, n = w.shape
    w = f64(np.asarray(w, np.float32).astype(ml_dtypes.bfloat16)).reshape(k // 32, 32, n)
    amax = np.abs(w).max(1)
    if fmt in ("e4m3", "e5m2"):
        byte = np.frexp(amax)[1] - 1 + 127 - (7 if fmt == "e4m3" else 14)
    else:
        mant, ex = np.frexp(amax / 6.0)
        byte = np.where(mant > 0.5, ex, ex - 1) + 127
    byte = np.clip(np.where(amax > 0, byte, 1), 1, 254)
    scaled = (w * np.exp2(127.0 - byte)[:, None, :]).reshape(k, n).astype(np.float32)
    by_word = np.ascontiguousarray(scaled.reshape(k // 512, 128, 4, n).transpose(0, 1, 3, 2))
    if fmt in ("e4m3", "e5m2"):
        words = by_word.astype(ml_dtypes.float8_e4m3fn if fmt == "e4m3" else ml_dtypes.float8_e5m2).view(np.uint8)
    else:
        c = by_word.astype(ml_dtypes.float4_e2m1fn).view(np.uint8) & 0xF
        words = (c[..., 0::2] | (c[..., 1::2] << 4)).reshape(k // 512, 128, 2 * n)
    return np.ascontiguousarray(words), np.ascontiguousarray(byte.astype(np.uint8).reshape(k // 512, 16, n))


def unpack_weight(words, scales, fmt):
    g, _, n = scales.shape
    words = np.ascontiguousarray(words).reshape(g, 128, n, -1)
    if fmt in ("e4m3", "e5m2"):
        vals = words.view(ml_dtypes.float8_e4m3fn if fmt == "e4m3" else ml_dtypes.float8_e5m2).astype(np.float64)
    else:
        nib = np.empty((g, 128, n, 4), np.uint8)
        nib[..., 0::2] = words & 0xF
        nib[..., 1::2] = words >> 4
        vals = E2M1[nib]
    vals = vals * np.repeat(np.exp2(scales.astype(np.float64) - 127.0), 8, axis=1)[..., None]
    return vals.transpose(0, 1, 3, 2).reshape(g * 512, n)


K, T, Z, J, R, C, N = 512, 1024, 1024, 256, 512, 512, 256


def setup_inputs():
    n = np.random.standard_normal
    idx = np.random.permutation(T)[:J]
    idx2 = np.random.permutation(Z)[:J]
    idx3 = np.random.permutation(C)[:J]
    idx4 = np.random.permutation(C)[:J]
    fk = mx_kscale(K)
    fr = mx_kscale(R)
    xtp = pack_weight(n((K, T)) / fk[:, None], "e5m2")
    xop = pack_weight(n((K, Z)) / fk[:, None], "e4m3")
    wp = pack_weight(n((K, R)) * 1 / np.sqrt(K) * fk[:, None] * fr, "e2m1")
    wbp = pack_weight(n((R, N)) * 1 / np.sqrt(R) / fr[:, None], "e2m1")
    return {
        "xt_words": xtp[0],
        "xt_scales": xtp[1],
        "xo_words": xop[0],
        "xo_scales": xop[1],
        "w_words": wp[0],
        "w_scales": wp[1],
        "wb_words": wbp[0],
        "wb_scales": wbp[1],
        "offs": striped(idx),
        "offs2": striped(idx2),
        "offs3": striped(idx3),
        "offs4": striped(idx4),
    }


def reference(xt_words, xt_scales, xo_words, xo_scales, w_words, w_scales, wb_words, wb_scales, offs, offs2, offs3, offs4):
    idx = unstriped(offs)
    idx2 = unstriped(offs2)
    idx3 = unstriped(offs3)
    idx4 = unstriped(offs4)
    xtu = unpack_weight(xt_words, xt_scales, "e5m2")
    xou = unpack_weight(xo_words, xo_scales, "e4m3")
    wu = unpack_weight(w_words, w_scales, "e2m1")
    wbu = unpack_weight(wb_words, wb_scales, "e2m1")
    xtidxg = xtu[:, idx]
    a = wu.T @ xtidxg
    xoidx2g = xou[:, idx2]
    b = wu.T @ xoidx2g
    pw = np.zeros((R, C))
    pw[:, idx3] = a
    hid = np.maximum(pw[:, idx4], b)
    hidq = mxq(hid, 0, "e4m3")
    y = wbu.T @ hidq
    return y

@@ -1,0 +1,160 @@
+from contextlib import ExitStack
+
+import concourse.mybir as mybir
+
+K, T, Z, J, R, C, N = 512, 1024, 1024, 256, 512, 512, 256
+FLOPS = 2 * (2 * K * R * J + R * N * J)
+
+F32 = mybir.dt.float32
+BF16 = mybir.dt.bfloat16
+I32 = mybir.dt.int32
+U32 = mybir.dt.uint32
+U16 = mybir.dt.uint16
+U8 = mybir.dt.uint8
+E4M3 = mybir.dt.float8_e4m3fn_x4
+E5M2 = mybir.dt.float8_e5m2_x4
+E2M1 = mybir.dt.float4_e2m1fn_x4
+COPY = mybir.ActivationFunctionType.Copy
+MAX = mybir.AluOpType.max
+
+P = 128
+PACK = 4
+HALF = J // 2
+LIST_COLS = J // 16
+
+
+def tile_list_oneforboth_board_one_plain_kernel(
+    tc, xt_words, xt_scales, xo_words, xo_scales, w_words, w_scales, wb_words, wb_scales,
+    offs, offs2, offs3, offs4, out,
+):
+    nc = tc.nc
+    with ExitStack() as ctx:
+        lists = ctx.enter_context(tc.tile_pool(name="lists", bufs=1))
+        sb = ctx.enter_context(tc.tile_pool(name="sb", bufs=1))
+        ps = ctx.enter_context(tc.psum_pool(name="ps", bufs=1))
+
+        tok_list = lists.tile([P, LIST_COLS], U16, name="tok_list")
+        note_list = lists.tile([P, LIST_COLS], U16, name="note_list")
+        put_list = lists.tile([P, LIST_COLS], U16, name="put_list")
+        get_list = lists.tile([P, LIST_COLS], U16, name="get_list")
+
+        xt_w = sb.tile([P, T], U32, name="xt_w", align_bytes=64)
+        xt_s = sb.tile([P, T], U8, name="xt_s", align_bytes=64)
+        xo_w = sb.tile([P, Z], U32, name="xo_w", align_bytes=64)
+        xo_s = sb.tile([P, Z], U8, name="xo_s", align_bytes=64)
+        w_w = sb.tile([P, R], U16, name="w_w", align_bytes=64)
+        w_s = sb.tile([P, R], U8, name="w_s", align_bytes=64)
+        wb_w = sb.tile([P, N], U16, name="wb_w", align_bytes=64)
+        wb_s = sb.tile([P, N], U8, name="wb_s", align_bytes=64)
+        board = [sb.tile([P, C], F32, name="board%d" % t, align_bytes=64) for t in range(PACK)]
+
+        for t in range(PACK):
+            nc.vector.memset(board[t][:], 0.0)
+
+        def load_scales(plane, scales, quadrants):
+            for q in quadrants:
+                nc.sync.dma_start(
+                    out=plane[32 * q : 32 * q + 32, :].bitcast(I32),
+                    in_=scales[0, 4 * q : 4 * q + 4, :].bitcast(I32).partition_broadcast(8),
+                )
+
+        def load_words8(tile, words):
+            nc.sync.dma_start(
+                out=tile[:].bitcast(I32), in_=words[0].rearrange("p c b -> p (c b)").bitcast(I32)
+            )
+
+        def load_words4(tile, words):
+            nc.sync.dma_start(out=tile[:].bitcast(I32), in_=words[0].bitcast(I32))
+
+        load_scales(w_s, w_scales, range(4))
+        load_words8(xt_w, xt_words)
+        load_words4(w_w, w_words)
+        nc.sync.dma_start(tok_list[:], offs)
+        load_scales(xt_s, xt_scales, range(4))
+        load_words8(xo_w, xo_words)
+        nc.sync.dma_start(put_list[:], offs3)
+        nc.sync.dma_start(note_list[:], offs2)
+        load_scales(xo_s, xo_scales, range(4))
+        nc.sync.dma_start(get_list[:], offs4)
+        load_words4(wb_w, wb_words)
+        load_scales(wb_s, wb_scales, range(4))
+
+        wp_w = sb.tile([P, PACK, P], U16, name="wp_w", align_bytes=64)
+        wp_s = sb.tile([P, PACK, P], U8, name="wp_s", align_bytes=64)
+        nc.vector.tensor_copy(out=wp_s[:], in_=w_s[:].rearrange("p (m t) -> p t m", t=PACK))
+        nc.vector.tensor_copy(out=wp_w[:], in_=w_w[:].rearrange("p (m t) -> p t m", t=PACK))
+
+        tok_w = sb.tile([P, J], U32, name="tok_w", align_bytes=64)
+        tok_s = sb.tile([P, J], U8, name="tok_s", align_bytes=64)
+        note_w = sb.tile([P, J], U32, name="note_w", align_bytes=64)
+        note_s = sb.tile([P, J], U8, name="note_s", align_bytes=64)
+        nc.vector.tensor_copy(out=tok_w[:], in_=xt_w[:].indirect(tok_list[:]))
+        nc.vector.tensor_copy(out=tok_s[:], in_=xt_s[:].indirect(tok_list[:]))
+
+        a_ps = [ps.tile([P, J], F32, name="a_ps%d" % t, tag="bank%d" % t) for t in range(PACK)]
+        for t in (0, 1, 2, 3):
+            nc.tensor.matmul_mx(
+                out=a_ps[t][:], lhsT=wp_w[:, t, :].bitcast(E2M1), lhsT_scale=wp_s[:, t, :],
+                rhs=tok_w[:].bitcast(E5M2), rhs_scale=tok_s[:], start=True, stop=True,
+            )
+
+        nc.vector.tensor_copy(out=note_w[:], in_=xo_w[:].indirect(note_list[:]))
+
+        a_sb = [sb.tile([P, J], F32, name="a_sb%d" % t, align_bytes=64) for t in range(PACK)]
+        picked = sb.tile([P, PACK, J], F32, name="picked", align_bytes=64)
+
+        nc.scalar.activation(out=a_sb[0][:], in_=a_ps[0][:], func=COPY)
+        nc.scalar.activation(out=board[0][:].indirect(put_list[:]), in_=a_sb[0][:], func=COPY)
+        nc.vector.tensor_copy(out=a_sb[1][:], in_=a_ps[1][:])
+        nc.vector.tensor_copy(out=a_sb[2][:], in_=a_ps[2][:])
+        nc.vector.tensor_copy(out=board[1][:].indirect(put_list[:]), in_=a_sb[1][:])
+        nc.scalar.activation(out=board[2][:].indirect(put_list[:]), in_=a_sb[2][:], func=COPY)
+        nc.vector.tensor_copy(out=a_sb[3][:], in_=a_ps[3][:])
+        nc.scalar.activation(out=board[3][:].indirect(put_list[:]), in_=a_sb[3][:], func=COPY)
+        nc.vector.tensor_copy(out=note_s[:], in_=xo_s[:].indirect(note_list[:]))
+
+        b_ps = [ps.tile([P, PACK, HALF], F32, name="b_ps%d" % h) for h in range(2)]
+        for h in range(2):
+            cols = slice(h * HALF, (h + 1) * HALF)
+            for t in range(PACK):
+                nc.tensor.matmul_mx(
+                    out=b_ps[h][:, t, :], lhsT=wp_w[:, t, :].bitcast(E2M1), lhsT_scale=wp_s[:, t, :],
+                    rhs=note_w[:, cols].bitcast(E4M3), rhs_scale=note_s[:, cols], start=True, stop=True,
+                )
+
+        for t in range(PACK - 1):
+            nc.vector.tensor_copy(out=picked[:, t, :], in_=board[t][:].indirect(get_list[:]))
+        last = PACK - 1
+        nc.vector.tensor_copy(
+            out=picked[:, last, :HALF], in_=board[last][:].indirect(get_list[:, : LIST_COLS // 2])
+        )
+        nc.scalar.activation(
+            out=picked[:, last, HALF:], in_=board[last][:].indirect(get_list[:, LIST_COLS // 2 :]), func=COPY
+        )
+
+        out_v = out.rearrange("(c p) j -> p c j", p=P)
+        hid = [sb.tile([P, HALF * PACK], BF16, name="hid%d" % h, align_bytes=64) for h in range(2)]
+        hid_w = [sb.tile([P, HALF], U32, name="hid_w%d" % h, align_bytes=64) for h in range(2)]
+        hid_s = [sb.tile([P, HALF], U8, name="hid_s%d" % h, align_bytes=64) for h in range(2)]
+        res = [sb.tile([P, 2, HALF], F32, name="res%d" % h, align_bytes=64) for h in range(2)]
+        for h in range(2):
+            cols = slice(h * HALF, (h + 1) * HALF)
+            nc.vector.tensor_tensor(
+                out=hid[h][:].rearrange("p (g i t) -> p g t i", i=4, t=PACK),
+                in0=picked[:, :, cols].rearrange("p t (g i) -> p g t i", i=4),
+                in1=b_ps[h][:].rearrange("p t (g i) -> p g t i", i=4),
+                op=MAX,
+            )
+            nc.vector.quantize_mx(out=hid_w[h][:].bitcast(E4M3), scales=hid_s[h][:], in_=hid[h][:])
+            for c in range(2):
+                ncols = slice(c * P, (c + 1) * P)
+                y_ps = ps.tile([P, HALF], F32, name="y_ps%d%d" % (h, c), tag="bank%d" % (2 * h + c))
+                nc.tensor.matmul_mx(
+                    out=y_ps[:], lhsT=wb_w[:, ncols].bitcast(E2M1), lhsT_scale=wb_s[:, ncols],
+                    rhs=hid_w[h][:].bitcast(E4M3), rhs_scale=hid_s[h][:], start=True, stop=True,
+                )
+                if h == 1 and c == 1:
+                    nc.vector.tensor_copy(out=res[h][:, c, :], in_=y_ps[:])
+                else:
+                    nc.scalar.activation(out=res[h][:, c, :], in_=y_ps[:], func=COPY)
+            nc.sync.dma_start(out=out_v[:, :, cols], in_=res[h][:])

@@ -51,45 +51,56 @@ def tile_list_oneforboth_board_one_plain_kernel(
         for t in range(PACK):
             nc.vector.memset(board[t][:], 0.0)
 
-        def load_scales(plane, scales, quadrants):
-            for q in quadrants:
-                nc.sync.dma_start(
-                    out=plane[32 * q : 32 * q + 32, :].bitcast(I32),
-                    in_=scales[0, 4 * q : 4 * q + 4, :].bitcast(I32).partition_broadcast(8),
-                )
+        def load_scales_low(queue, plane, scales):
+            queue.dma_start(
+                out=plane[:16, :].bitcast(I32),
+                in_=scales[0, :4, :].bitcast(I32).partition_broadcast(4),
+            )
 
-        def load_words8(tile, words):
-            nc.sync.dma_start(
+        def load_scales_high(queue, plane, scales):
+            queue.dma_start(
+                out=plane[16:, :].bitcast(I32),
+                in_=scales[0, 2:, :].bitcast(I32).partition_broadcast(8),
+            )
+
+        def load_words8(queue, tile, words):
+            queue.dma_start(
                 out=tile[:].bitcast(I32), in_=words[0].rearrange("p c b -> p (c b)").bitcast(I32)
             )
 
-        def load_words4(tile, words):
-            nc.sync.dma_start(out=tile[:].bitcast(I32), in_=words[0].bitcast(I32))
+        def load_words4(queue, tile, words):
+            queue.dma_start(out=tile[:].bitcast(I32), in_=words[0].bitcast(I32))
 
-        load_scales(w_s, w_scales, range(4))
-        load_words8(xt_w, xt_words)
-        load_words4(w_w, w_words)
         nc.sync.dma_start(tok_list[:], offs)
-        load_scales(xt_s, xt_scales, range(4))
-        load_words8(xo_w, xo_words)
-        nc.sync.dma_start(put_list[:], offs3)
+        load_words4(nc.scalar, w_w, w_words)
+        load_words8(nc.sync, xt_w, xt_words)
+        load_scales_high(nc.scalar, xt_s, xt_scales)
+        load_scales_low(nc.scalar, w_s, w_scales)
+        load_scales_low(nc.scalar, xt_s, xt_scales)
+        load_scales_high(nc.sync, w_s, w_scales)
         nc.sync.dma_start(note_list[:], offs2)
-        load_scales(xo_s, xo_scales, range(4))
+        load_words8(nc.sync, xo_w, xo_words)
+        load_scales_high(nc.sync, xo_s, xo_scales)
+        load_scales_low(nc.sync, xo_s, xo_scales)
+        nc.sync.dma_start(put_list[:], offs3)
         nc.sync.dma_start(get_list[:], offs4)
-        load_words4(wb_w, wb_words)
-        load_scales(wb_s, wb_scales, range(4))
+        load_words4(nc.sync, wb_w, wb_words)
+        load_scales_low(nc.sync, wb_s, wb_scales)
+        load_scales_high(nc.sync, wb_s, wb_scales)
 
         wp_w = sb.tile([P, PACK, P], U16, name="wp_w", align_bytes=64)
         wp_s = sb.tile([P, PACK, P], U8, name="wp_s", align_bytes=64)
-        nc.vector.tensor_copy(out=wp_s[:], in_=w_s[:].rearrange("p (m t) -> p t m", t=PACK))
         nc.vector.tensor_copy(out=wp_w[:], in_=w_w[:].rearrange("p (m t) -> p t m", t=PACK))
 
         tok_w = sb.tile([P, J], U32, name="tok_w", align_bytes=64)
         tok_s = sb.tile([P, J], U8, name="tok_s", align_bytes=64)
         note_w = sb.tile([P, J], U32, name="note_w", align_bytes=64)
         note_s = sb.tile([P, J], U8, name="note_s", align_bytes=64)
-        nc.vector.tensor_copy(out=tok_w[:], in_=xt_w[:].indirect(tok_list[:]))
         nc.vector.tensor_copy(out=tok_s[:], in_=xt_s[:].indirect(tok_list[:]))
+        nc.vector.tensor_copy(out=tok_w[:], in_=xt_w[:].indirect(tok_list[:]))
+        w_s_dealt = w_s[:].rearrange("p (m t) -> p t m", t=PACK)
+        nc.vector.tensor_copy(out=wp_s[:, 0, :], in_=w_s_dealt[:, 0, :])
+        nc.vector.tensor_copy(out=wp_s[:, 1:, :], in_=w_s_dealt[:, 1:, :])
 
         a_ps = [ps.tile([P, J], F32, name="a_ps%d" % t, tag="bank%d" % t) for t in range(PACK)]
         for t in (0, 1, 2, 3):
@@ -99,19 +110,15 @@ def tile_list_oneforboth_board_one_plain_kernel(
             )
 
         nc.vector.tensor_copy(out=note_w[:], in_=xo_w[:].indirect(note_list[:]))
+        nc.vector.tensor_copy(out=note_s[:], in_=xo_s[:].indirect(note_list[:]))
 
         a_sb = [sb.tile([P, J], F32, name="a_sb%d" % t, align_bytes=64) for t in range(PACK)]
-        picked = sb.tile([P, PACK, J], F32, name="picked", align_bytes=64)
-
-        nc.scalar.activation(out=a_sb[0][:], in_=a_ps[0][:], func=COPY)
-        nc.scalar.activation(out=board[0][:].indirect(put_list[:]), in_=a_sb[0][:], func=COPY)
-        nc.vector.tensor_copy(out=a_sb[1][:], in_=a_ps[1][:])
-        nc.vector.tensor_copy(out=a_sb[2][:], in_=a_ps[2][:])
-        nc.vector.tensor_copy(out=board[1][:].indirect(put_list[:]), in_=a_sb[1][:])
-        nc.scalar.activation(out=board[2][:].indirect(put_list[:]), in_=a_sb[2][:], func=COPY)
-        nc.vector.tensor_copy(out=a_sb[3][:], in_=a_ps[3][:])
-        nc.scalar.activation(out=board[3][:].indirect(put_list[:]), in_=a_sb[3][:], func=COPY)
-        nc.vector.tensor_copy(out=note_s[:], in_=xo_s[:].indirect(note_list[:]))
+        picked = [sb.tile([P, PACK, HALF], F32, name="picked%d" % h, align_bytes=64) for h in range(2)]
+        for t in (0, 1, 2, 3):
+            nc.scalar.activation(out=a_sb[t][:], in_=a_ps[t][:], func=COPY)
+        for t in (0, 2):
+            nc.vector.tensor_copy(out=board[t][:].indirect(put_list[:]), in_=a_sb[t][:])
+            nc.scalar.activation(out=board[t + 1][:].indirect(put_list[:]), in_=a_sb[t + 1][:], func=COPY)
 
         b_ps = [ps.tile([P, PACK, HALF], F32, name="b_ps%d" % h) for h in range(2)]
         for h in range(2):
@@ -122,15 +129,16 @@ def tile_list_oneforboth_board_one_plain_kernel(
                     rhs=note_w[:, cols].bitcast(E4M3), rhs_scale=note_s[:, cols], start=True, stop=True,
                 )
 
-        for t in range(PACK - 1):
-            nc.vector.tensor_copy(out=picked[:, t, :], in_=board[t][:].indirect(get_list[:]))
-        last = PACK - 1
-        nc.vector.tensor_copy(
-            out=picked[:, last, :HALF], in_=board[last][:].indirect(get_list[:, : LIST_COLS // 2])
-        )
-        nc.scalar.activation(
-            out=picked[:, last, HALF:], in_=board[last][:].indirect(get_list[:, LIST_COLS // 2 :]), func=COPY
-        )
+        def pick(t, h):
+            half_list = get_list[:, h * LIST_COLS // 2 : (h + 1) * LIST_COLS // 2]
+            return picked[h][:, t, :], board[t][:].indirect(half_list)
+
+        for t, h in ((1, 1), (3, 0), (3, 1)):
+            dst, src = pick(t, h)
+            nc.scalar.activation(out=dst, in_=src, func=COPY)
+        for t, h in ((0, 0), (2, 0), (1, 0), (0, 1), (2, 1)):
+            dst, src = pick(t, h)
+            nc.vector.tensor_copy(out=dst, in_=src)
 
         out_v = out.rearrange("(c p) j -> p c j", p=P)
         hid = [sb.tile([P, HALF * PACK], BF16, name="hid%d" % h, align_bytes=64) for h in range(2)]
@@ -141,7 +149,7 @@ def tile_list_oneforboth_board_one_plain_kernel(
             cols = slice(h * HALF, (h + 1) * HALF)
             nc.vector.tensor_tensor(
                 out=hid[h][:].rearrange("p (g i t) -> p g t i", i=4, t=PACK),
-                in0=picked[:, :, cols].rearrange("p t (g i) -> p g t i", i=4),
+                in0=picked[h][:].rearrange("p t (g i) -> p g t i", i=4),
                 in1=b_ps[h][:].rearrange("p t (g i) -> p g t i", i=4),
                 op=MAX,
             )

@@ -54,7 +54,7 @@ def tile_list_oneforboth_board_one_plain_kernel(
         def load_scales_low(queue, plane, scales):
             queue.dma_start(
                 out=plane[:16, :].bitcast(I32),
-                in_=scales[0, :4, :].bitcast(I32).partition_broadcast(4),
+                in_=scales[0].bitcast(I32),
             )
 
         def load_scales_high(queue, plane, scales):
@@ -73,12 +73,12 @@ def tile_list_oneforboth_board_one_plain_kernel(
 
         nc.sync.dma_start(tok_list[:], offs)
         load_words4(nc.scalar, w_w, w_words)
+        nc.sync.dma_start(note_list[:], offs2)
         load_words8(nc.sync, xt_w, xt_words)
         load_scales_high(nc.scalar, xt_s, xt_scales)
         load_scales_low(nc.scalar, w_s, w_scales)
         load_scales_low(nc.scalar, xt_s, xt_scales)
         load_scales_high(nc.sync, w_s, w_scales)
-        nc.sync.dma_start(note_list[:], offs2)
         load_words8(nc.sync, xo_w, xo_words)
         load_scales_high(nc.sync, xo_s, xo_scales)
         load_scales_low(nc.sync, xo_s, xo_scales)
@@ -89,7 +89,6 @@ def tile_list_oneforboth_board_one_plain_kernel(
         load_scales_high(nc.sync, wb_s, wb_scales)
 
         wp_w = sb.tile([P, PACK, P], U16, name="wp_w", align_bytes=64)
-        wp_s = sb.tile([P, PACK, P], U8, name="wp_s", align_bytes=64)
         nc.vector.tensor_copy(out=wp_w[:], in_=w_w[:].rearrange("p (m t) -> p t m", t=PACK))
 
         tok_w = sb.tile([P, J], U32, name="tok_w", align_bytes=64)
@@ -98,6 +97,7 @@ def tile_list_oneforboth_board_one_plain_kernel(
         note_s = sb.tile([P, J], U8, name="note_s", align_bytes=64)
         nc.vector.tensor_copy(out=tok_s[:], in_=xt_s[:].indirect(tok_list[:]))
         nc.vector.tensor_copy(out=tok_w[:], in_=xt_w[:].indirect(tok_list[:]))
+        wp_s = sb.tile([P, PACK, P], U8, name="wp_s", tag="xt_w", align_bytes=64)
         w_s_dealt = w_s[:].rearrange("p (m t) -> p t m", t=PACK)
         nc.vector.tensor_copy(out=wp_s[:, 0, :], in_=w_s_dealt[:, 0, :])
         nc.vector.tensor_copy(out=wp_s[:, 1:, :], in_=w_s_dealt[:, 1:, :])
@@ -140,7 +140,6 @@ def tile_list_oneforboth_board_one_plain_kernel(
             dst, src = pick(t, h)
             nc.vector.tensor_copy(out=dst, in_=src)
 
-        out_v = out.rearrange("(c p) j -> p c j", p=P)
         hid = [sb.tile([P, HALF * PACK], BF16, name="hid%d" % h, align_bytes=64) for h in range(2)]
         hid_w = [sb.tile([P, HALF], U32, name="hid_w%d" % h, align_bytes=64) for h in range(2)]
         hid_s = [sb.tile([P, HALF], U8, name="hid_s%d" % h, align_bytes=64) for h in range(2)]
@@ -165,4 +164,4 @@ def tile_list_oneforboth_board_one_plain_kernel(
                     nc.vector.tensor_copy(out=res[h][:, c, :], in_=y_ps[:])
                 else:
                     nc.scalar.activation(out=res[h][:, c, :], in_=y_ps[:], func=COPY)
-            nc.sync.dma_start(out=out_v[:, :, cols], in_=res[h][:])
+                nc.sync.dma_start(out=out[ncols, cols], in_=res[h][:, c, :])

@@ -48,6 +48,7 @@ def tile_list_oneforboth_board_one_plain_kernel(
         wb_s = sb.tile([P, N], U8, name="wb_s", align_bytes=64)
         board = [sb.tile([P, C], F32, name="board%d" % t, align_bytes=64) for t in range(PACK)]
 
+        nc.vector.memset(xt_s[:].bitcast(I32), 0)
         for t in range(PACK):
             nc.vector.memset(board[t][:], 0.0)
 
@@ -73,22 +74,26 @@ def tile_list_oneforboth_board_one_plain_kernel(
 
         nc.sync.dma_start(tok_list[:], offs)
         load_words4(nc.scalar, w_w, w_words)
-        nc.sync.dma_start(note_list[:], offs2)
         load_words8(nc.sync, xt_w, xt_words)
-        load_scales_high(nc.scalar, xt_s, xt_scales)
-        load_scales_low(nc.scalar, w_s, w_scales)
-        load_scales_low(nc.scalar, xt_s, xt_scales)
+        for q in range(4):
+            nc.scalar.dma_start(
+                out=xt_s[32 * q : 32 * q + 4, :].bitcast(I32),
+                in_=xt_scales[0, 4 * q : 4 * q + 4, :].bitcast(I32),
+            )
         load_scales_high(nc.sync, w_s, w_scales)
+        load_scales_low(nc.sync, w_s, w_scales)
+        nc.sync.dma_start(put_list[:], offs3)
         load_words8(nc.sync, xo_w, xo_words)
+        nc.sync.dma_start(note_list[:], offs2)
         load_scales_high(nc.sync, xo_s, xo_scales)
         load_scales_low(nc.sync, xo_s, xo_scales)
-        nc.sync.dma_start(put_list[:], offs3)
         nc.sync.dma_start(get_list[:], offs4)
         load_words4(nc.sync, wb_w, wb_words)
         load_scales_low(nc.sync, wb_s, wb_scales)
         load_scales_high(nc.sync, wb_s, wb_scales)
 
         wp_w = sb.tile([P, PACK, P], U16, name="wp_w", align_bytes=64)
+        wp_s = sb.tile([P, PACK, P], U8, name="wp_s", align_bytes=64)
         nc.vector.tensor_copy(out=wp_w[:], in_=w_w[:].rearrange("p (m t) -> p t m", t=PACK))
 
         tok_w = sb.tile([P, J], U32, name="tok_w", align_bytes=64)
@@ -97,7 +102,6 @@ def tile_list_oneforboth_board_one_plain_kernel(
         note_s = sb.tile([P, J], U8, name="note_s", align_bytes=64)
         nc.vector.tensor_copy(out=tok_s[:], in_=xt_s[:].indirect(tok_list[:]))
         nc.vector.tensor_copy(out=tok_w[:], in_=xt_w[:].indirect(tok_list[:]))
-        wp_s = sb.tile([P, PACK, P], U8, name="wp_s", tag="xt_w", align_bytes=64)
         w_s_dealt = w_s[:].rearrange("p (m t) -> p t m", t=PACK)
         nc.vector.tensor_copy(out=wp_s[:, 0, :], in_=w_s_dealt[:, 0, :])
         nc.vector.tensor_copy(out=wp_s[:, 1:, :], in_=w_s_dealt[:, 1:, :])
@@ -109,16 +113,16 @@ def tile_list_oneforboth_board_one_plain_kernel(
                 rhs=tok_w[:].bitcast(E5M2), rhs_scale=tok_s[:], start=True, stop=True,
             )
 
-        nc.vector.tensor_copy(out=note_w[:], in_=xo_w[:].indirect(note_list[:]))
-        nc.vector.tensor_copy(out=note_s[:], in_=xo_s[:].indirect(note_list[:]))
-
         a_sb = [sb.tile([P, J], F32, name="a_sb%d" % t, align_bytes=64) for t in range(PACK)]
         picked = [sb.tile([P, PACK, HALF], F32, name="picked%d" % h, align_bytes=64) for h in range(2)]
-        for t in (0, 1, 2, 3):
+        nc.vector.tensor_copy(out=a_sb[0][:], in_=a_ps[0][:])
+        for t in range(1, PACK):
             nc.scalar.activation(out=a_sb[t][:], in_=a_ps[t][:], func=COPY)
         for t in (0, 2):
             nc.vector.tensor_copy(out=board[t][:].indirect(put_list[:]), in_=a_sb[t][:])
             nc.scalar.activation(out=board[t + 1][:].indirect(put_list[:]), in_=a_sb[t + 1][:], func=COPY)
+        nc.vector.tensor_copy(out=note_w[:], in_=xo_w[:].indirect(note_list[:]))
+        nc.vector.tensor_copy(out=note_s[:], in_=xo_s[:].indirect(note_list[:]))
 
         b_ps = [ps.tile([P, PACK, HALF], F32, name="b_ps%d" % h) for h in range(2)]
         for h in range(2):
@@ -133,10 +137,10 @@ def tile_list_oneforboth_board_one_plain_kernel(
             half_list = get_list[:, h * LIST_COLS // 2 : (h + 1) * LIST_COLS // 2]
             return picked[h][:, t, :], board[t][:].indirect(half_list)
 
-        for t, h in ((1, 1), (3, 0), (3, 1)):
+        for t, h in ((1, 0), (0, 0), (3, 0), (1, 1), (3, 1)):
             dst, src = pick(t, h)
             nc.scalar.activation(out=dst, in_=src, func=COPY)
-        for t, h in ((0, 0), (2, 0), (1, 0), (0, 1), (2, 1)):
+        for t, h in ((2, 0), (0, 1), (2, 1)):
             dst, src = pick(t, h)
             nc.vector.tensor_copy(out=dst, in_=src)
 

@@ -50,7 +50,7 @@ def tile_list_oneforboth_board_one_plain_kernel(
 
         nc.vector.memset(xt_s[:].bitcast(I32), 0)
         for t in range(PACK):
-            nc.vector.memset(board[t][:], 0.0)
+            nc.vector.memset(board[t][:].bitcast(I32), 0)
 
         def load_scales_low(queue, plane, scales):
             queue.dma_start(
@@ -82,9 +82,9 @@ def tile_list_oneforboth_board_one_plain_kernel(
             )
         load_scales_high(nc.sync, w_s, w_scales)
         load_scales_low(nc.sync, w_s, w_scales)
-        nc.sync.dma_start(put_list[:], offs3)
         load_words8(nc.sync, xo_w, xo_words)
         nc.sync.dma_start(note_list[:], offs2)
+        nc.sync.dma_start(put_list[:], offs3)
         load_scales_high(nc.sync, xo_s, xo_scales)
         load_scales_low(nc.sync, xo_s, xo_scales)
         nc.sync.dma_start(get_list[:], offs4)
@@ -94,7 +94,7 @@ def tile_list_oneforboth_board_one_plain_kernel(
 
         wp_w = sb.tile([P, PACK, P], U16, name="wp_w", align_bytes=64)
         wp_s = sb.tile([P, PACK, P], U8, name="wp_s", align_bytes=64)
-        nc.vector.tensor_copy(out=wp_w[:], in_=w_w[:].rearrange("p (m t) -> p t m", t=PACK))
+        nc.scalar.copy(out=wp_w[:], in_=w_w[:].rearrange("p (m t) -> p t m", t=PACK))
 
         tok_w = sb.tile([P, J], U32, name="tok_w", align_bytes=64)
         tok_s = sb.tile([P, J], U8, name="tok_s", align_bytes=64)
@@ -115,13 +115,12 @@ def tile_list_oneforboth_board_one_plain_kernel(
 
         a_sb = [sb.tile([P, J], F32, name="a_sb%d" % t, align_bytes=64) for t in range(PACK)]
         picked = [sb.tile([P, PACK, HALF], F32, name="picked%d" % h, align_bytes=64) for h in range(2)]
-        nc.vector.tensor_copy(out=a_sb[0][:], in_=a_ps[0][:])
-        for t in range(1, PACK):
+        nc.vector.tensor_copy(out=note_w[:], in_=xo_w[:].indirect(note_list[:]))
+        for t in range(PACK):
             nc.scalar.activation(out=a_sb[t][:], in_=a_ps[t][:], func=COPY)
         for t in (0, 2):
             nc.vector.tensor_copy(out=board[t][:].indirect(put_list[:]), in_=a_sb[t][:])
             nc.scalar.activation(out=board[t + 1][:].indirect(put_list[:]), in_=a_sb[t + 1][:], func=COPY)
-        nc.vector.tensor_copy(out=note_w[:], in_=xo_w[:].indirect(note_list[:]))
         nc.vector.tensor_copy(out=note_s[:], in_=xo_s[:].indirect(note_list[:]))
 
         b_ps = [ps.tile([P, PACK, HALF], F32, name="b_ps%d" % h) for h in range(2)]
@@ -137,10 +136,10 @@ def tile_list_oneforboth_board_one_plain_kernel(
             half_list = get_list[:, h * LIST_COLS // 2 : (h + 1) * LIST_COLS // 2]
             return picked[h][:, t, :], board[t][:].indirect(half_list)
 
-        for t, h in ((1, 0), (0, 0), (3, 0), (1, 1), (3, 1)):
+        for t, h in ((1, 0), (3, 0), (1, 1), (3, 1)):
             dst, src = pick(t, h)
             nc.scalar.activation(out=dst, in_=src, func=COPY)
-        for t, h in ((2, 0), (0, 1), (2, 1)):
+        for t, h in ((0, 0), (2, 0), (0, 1), (2, 1)):
             dst, src = pick(t, h)
             nc.vector.tensor_copy(out=dst, in_=src)
 

from contextlib import ExitStack

import concourse.mybir as mybir

K, T, Z, J, R, C, N = 512, 1024, 1024, 256, 512, 512, 256
FLOPS = 2 * (2 * K * R * J + R * N * J)

F32 = mybir.dt.float32
BF16 = mybir.dt.bfloat16
I32 = mybir.dt.int32
U32 = mybir.dt.uint32
U16 = mybir.dt.uint16
U8 = mybir.dt.uint8
E4M3 = mybir.dt.float8_e4m3fn_x4
E5M2 = mybir.dt.float8_e5m2_x4
E2M1 = mybir.dt.float4_e2m1fn_x4
COPY = mybir.ActivationFunctionType.Copy
MAX = mybir.AluOpType.max

P = 128
PACK = 4
HALF = J // 2
LIST_COLS = J // 16


def tile_list_oneforboth_board_one_plain_kernel(
    tc, xt_words, xt_scales, xo_words, xo_scales, w_words, w_scales, wb_words, wb_scales,
    offs, offs2, offs3, offs4, out,
):
    nc = tc.nc
    with ExitStack() as ctx:
        lists = ctx.enter_context(tc.tile_pool(name="lists", bufs=1))
        sb = ctx.enter_context(tc.tile_pool(name="sb", bufs=1))
        ps = ctx.enter_context(tc.psum_pool(name="ps", bufs=1))

        tok_list = lists.tile([P, LIST_COLS], U16, name="tok_list")
        note_list = lists.tile([P, LIST_COLS], U16, name="note_list")
        put_list = lists.tile([P, LIST_COLS], U16, name="put_list")
        get_list = lists.tile([P, LIST_COLS], U16, name="get_list")

        xt_w = sb.tile([P, T], U32, name="xt_w", align_bytes=64)
        xt_s = sb.tile([P, T], U8, name="xt_s", align_bytes=64)
        xo_w = sb.tile([P, Z], U32, name="xo_w", align_bytes=64)
        xo_s = sb.tile([P, Z], U8, name="xo_s", align_bytes=64)
        w_w = sb.tile([P, R], U16, name="w_w", align_bytes=64)
        w_s = sb.tile([P, R], U8, name="w_s", align_bytes=64)
        wb_w = sb.tile([P, N], U16, name="wb_w", align_bytes=64)
        wb_s = sb.tile([P, N], U8, name="wb_s", align_bytes=64)
        board = [sb.tile([P, C], F32, name="board%d" % t, align_bytes=64) for t in range(PACK)]

        nc.vector.memset(xt_s[:].bitcast(I32), 0)
        for t in range(PACK):
            nc.vector.memset(board[t][:].bitcast(I32), 0)

        def load_scales_low(queue, plane, scales):
            queue.dma_start(
                out=plane[:16, :].bitcast(I32),
                in_=scales[0].bitcast(I32),
            )

        def load_scales_high(queue, plane, scales):
            queue.dma_start(
                out=plane[16:, :].bitcast(I32),
                in_=scales[0, 2:, :].bitcast(I32).partition_broadcast(8),
            )

        def load_words8(queue, tile, words):
            queue.dma_start(
                out=tile[:].bitcast(I32), in_=words[0].rearrange("p c b -> p (c b)").bitcast(I32)
            )

        def load_words4(queue, tile, words):
            queue.dma_start(out=tile[:].bitcast(I32), in_=words[0].bitcast(I32))

        nc.sync.dma_start(tok_list[:], offs)
        load_words4(nc.scalar, w_w, w_words)
        load_words8(nc.sync, xt_w, xt_words)
        for q in range(4):
            nc.scalar.dma_start(
                out=xt_s[32 * q : 32 * q + 4, :].bitcast(I32),
                in_=xt_scales[0, 4 * q : 4 * q + 4, :].bitcast(I32),
            )
        load_scales_high(nc.sync, w_s, w_scales)
        load_scales_low(nc.sync, w_s, w_scales)
        load_words8(nc.sync, xo_w, xo_words)
        nc.sync.dma_start(note_list[:], offs2)
        nc.sync.dma_start(put_list[:], offs3)
        load_scales_high(nc.sync, xo_s, xo_scales)
        load_scales_low(nc.sync, xo_s, xo_scales)
        nc.sync.dma_start(get_list[:], offs4)
        load_words4(nc.sync, wb_w, wb_words)
        load_scales_low(nc.sync, wb_s, wb_scales)
        load_scales_high(nc.sync, wb_s, wb_scales)

        wp_w = sb.tile([P, PACK, P], U16, name="wp_w", align_bytes=64)
        wp_s = sb.tile([P, PACK, P], U8, name="wp_s", align_bytes=64)
        nc.scalar.copy(out=wp_w[:], in_=w_w[:].rearrange("p (m t) -> p t m", t=PACK))

        tok_w = sb.tile([P, J], U32, name="tok_w", align_bytes=64)
        tok_s = sb.tile([P, J], U8, name="tok_s", align_bytes=64)
        note_w = sb.tile([P, J], U32, name="note_w", align_bytes=64)
        note_s = sb.tile([P, J], U8, name="note_s", align_bytes=64)
        nc.vector.tensor_copy(out=tok_s[:], in_=xt_s[:].indirect(tok_list[:]))
        nc.vector.tensor_copy(out=tok_w[:], in_=xt_w[:].indirect(tok_list[:]))
        w_s_dealt = w_s[:].rearrange("p (m t) -> p t m", t=PACK)
        nc.vector.tensor_copy(out=wp_s[:, 0, :], in_=w_s_dealt[:, 0, :])
        nc.vector.tensor_copy(out=wp_s[:, 1:, :], in_=w_s_dealt[:, 1:, :])

        a_ps = [ps.tile([P, J], F32, name="a_ps%d" % t, tag="bank%d" % t) for t in range(PACK)]
        for t in (0, 1, 2, 3):
            nc.tensor.matmul_mx(
                out=a_ps[t][:], lhsT=wp_w[:, t, :].bitcast(E2M1), lhsT_scale=wp_s[:, t, :],
                rhs=tok_w[:].bitcast(E5M2), rhs_scale=tok_s[:], start=True, stop=True,
            )

        a_sb = [sb.tile([P, J], F32, name="a_sb%d" % t, align_bytes=64) for t in range(PACK)]
        picked = [sb.tile([P, PACK, HALF], F32, name="picked%d" % h, align_bytes=64) for h in range(2)]
        nc.vector.tensor_copy(out=note_w[:], in_=xo_w[:].indirect(note_list[:]))
        for t in range(PACK):
            nc.scalar.activation(out=a_sb[t][:], in_=a_ps[t][:], func=COPY)
        for t in (0, 2):
            nc.vector.tensor_copy(out=board[t][:].indirect(put_list[:]), in_=a_sb[t][:])
            nc.scalar.activation(out=board[t + 1][:].indirect(put_list[:]), in_=a_sb[t + 1][:], func=COPY)
        nc.vector.tensor_copy(out=note_s[:], in_=xo_s[:].indirect(note_list[:]))

        b_ps = [ps.tile([P, PACK, HALF], F32, name="b_ps%d" % h) for h in range(2)]
        for h in range(2):
            cols = slice(h * HALF, (h + 1) * HALF)
            for t in range(PACK):
                nc.tensor.matmul_mx(
                    out=b_ps[h][:, t, :], lhsT=wp_w[:, t, :].bitcast(E2M1), lhsT_scale=wp_s[:, t, :],
                    rhs=note_w[:, cols].bitcast(E4M3), rhs_scale=note_s[:, cols], start=True, stop=True,
                )

        def pick(t, h):
            half_list = get_list[:, h * LIST_COLS // 2 : (h + 1) * LIST_COLS // 2]
            return picked[h][:, t, :], board[t][:].indirect(half_list)

        for t, h in ((1, 0), (3, 0), (1, 1), (3, 1)):
            dst, src = pick(t, h)
            nc.scalar.activation(out=dst, in_=src, func=COPY)
        for t, h in ((0, 0), (2, 0), (0, 1), (2, 1)):
            dst, src = pick(t, h)
            nc.vector.tensor_copy(out=dst, in_=src)

        hid = [sb.tile([P, HALF * PACK], BF16, name="hid%d" % h, align_bytes=64) for h in range(2)]
        hid_w = [sb.tile([P, HALF], U32, name="hid_w%d" % h, align_bytes=64) for h in range(2)]
        hid_s = [sb.tile([P, HALF], U8, name="hid_s%d" % h, align_bytes=64) for h in range(2)]
        res = [sb.tile([P, 2, HALF], F32, name="res%d" % h, align_bytes=64) for h in range(2)]
        for h in range(2):
            cols = slice(h * HALF, (h + 1) * HALF)
            nc.vector.tensor_tensor(
                out=hid[h][:].rearrange("p (g i t) -> p g t i", i=4, t=PACK),
                in0=picked[h][:].rearrange("p t (g i) -> p g t i", i=4),
                in1=b_ps[h][:].rearrange("p t (g i) -> p g t i", i=4),
                op=MAX,
            )
            nc.vector.quantize_mx(out=hid_w[h][:].bitcast(E4M3), scales=hid_s[h][:], in_=hid[h][:])
            for c in range(2):
                ncols = slice(c * P, (c + 1) * P)
                y_ps = ps.tile([P, HALF], F32, name="y_ps%d%d" % (h, c), tag="bank%d" % (2 * h + c))
                nc.tensor.matmul_mx(
                    out=y_ps[:], lhsT=wb_w[:, ncols].bitcast(E2M1), lhsT_scale=wb_s[:, ncols],
                    rhs=hid_w[h][:].bitcast(E4M3), rhs_scale=hid_s[h][:], start=True, stop=True,
                )
                if h == 1 and c == 1:
                    nc.vector.tensor_copy(out=res[h][:, c, :], in_=y_ps[:])
                else:
                    nc.scalar.activation(out=res[h][:, c, :], in_=y_ps[:], func=COPY)
                nc.sync.dma_start(out=out[ncols, cols], in_=res[h][:, c, :])
